import numpy as np
import ml_dtypes


def mxq(x, axis, fmt="e4m3"):
    dtype, down = {"e4m3": (ml_dtypes.float8_e4m3fn, 7), "e5m2": (ml_dtypes.float8_e5m2, 14)}[fmt]
    v = np.moveaxis(np.asarray(x, np.float32).astype(ml_dtypes.bfloat16).astype(np.float64), axis, -1)
    blocks = v.reshape(v.shape[:-1] + (-1, 32))
    amax = np.abs(blocks).max(-1, keepdims=True)
    byte = np.maximum(np.where(amax > 0, np.frexp(amax)[1] - 1 + 127, 0) - down, 1)
    scale = np.exp2(byte - 127.0)
    codes = (blocks / scale).astype(np.float32).astype(dtype).astype(np.float64)
    return np.moveaxis((codes * scale).reshape(v.shape), -1, axis)


WIDE = False


def mx_kscale(k):
    if not WIDE:
        return np.ones(k)
    levels = np.array([10, -10, 5, -5, 0])
    if k % 512:
        return np.exp2(np.random.permutation(np.resize(levels, k // 32))).repeat(32)
    a = np.empty((k // 512, 16))
    for p in range(k // 512):
        a[p, :8] = np.random.permutation(np.resize(levels, 8))
        for g in range(8):
            far = levels[np.abs(levels - a[p, g]) >= 10]
            a[p, g + 8] = far[np.random.randint(len(far))]
    return np.exp2(a.ravel()).repeat(32)


def f64(x):
    return np.asarray(x).astype(np.float64)


def striped(idx):
    return np.tile(idx.reshape(-1, 16).T, (8, 1)).astype(np.uint16)


def unstriped(offs):
    return offs[:16].T.reshape(-1).astype(np.int64)


def striped8(idx):
    return np.concatenate([x.reshape(-1, 16).T for x in idx]).astype(np.uint16)


def runs(offs, k):
    lists = np.stack([offs[16 * r : 16 * r + 16].T.reshape(-1) for r in range(8)]).astype(np.int64)
    return lists[np.arange(k) % 512 // 64]


def pack_weight(w):
    k, n = w.shape
    w = f64(np.asarray(w, np.float32).astype(ml_dtypes.bfloat16)).reshape(k // 32, 32, n)
    amax = np.abs(w).max(1)
    byte = np.clip(np.where(amax > 0, np.frexp(amax)[1] - 1 + 127 - 7, 1), 1, 254)
    scaled = (w * np.exp2(127.0 - byte)[:, None, :]).reshape(k, n).astype(np.float32)
    words = np.ascontiguousarray(scaled.reshape(k // 512, 128, 4, n).transpose(0, 1, 3, 2)).astype(ml_dtypes.float8_e4m3fn).view(np.uint8)
    return words, np.ascontiguousarray(byte.astype(np.uint8).reshape(k // 512, 16, n))


def unpack_weight(words, scales):
    g, p, n, _ = words.shape
    vals = np.ascontiguousarray(words).view(ml_dtypes.float8_e4m3fn).astype(np.float64) * np.repeat(np.exp2(scales.astype(np.float64) - 127.0), 8, axis=1)[..., None]
    return vals.transpose(0, 1, 3, 2).reshape(g * 512, n)


def relu(v):
    return np.maximum(v, 0.0)


K, T, S, V, H = 512, 2048, 512, 512, 512


def setup_inputs():
    n = np.random.standard_normal
    s = mx_kscale(K)[:, None]
    u = mx_kscale(S)
    packed_xT = pack_weight(n((K, T)) * s)
    return {
        "x_words": packed_xT[0],
        "x_scales": packed_xT[1],
        "w1": (n((K, H)) / np.sqrt(K) / s).astype(np.float32),
        "w2": (n((K, H)) / np.sqrt(K) / s).astype(np.float32),
        "ga": (np.random.uniform(0.5, 1.5, (H, 1)) * u[:, None]).astype(np.float32),
        "gb": (np.random.uniform(0.5, 1.5, (H, 1)) / u[:, None]).astype(np.float32),
        "offs": striped8(np.random.randint(0, T, (8, S))),
        "two": striped(np.random.permutation(T)[:V]),
        "n1": striped(np.random.permutation(S)),
        "n2": striped(np.random.permutation(S)),
        "n3": striped(np.random.permutation(V)),
        "n4": striped(np.random.permutation(V)),
        "n5": striped(np.random.permutation(V)),
        "n6": striped(np.random.permutation(V)),
    }


def reference(x_words, x_scales, w1, w2, ga, gb, offs, two, n1, n2, n3, n4, n5, n6):
    xq = unpack_weight(x_words, x_scales)[np.arange(K)[:, None], runs(offs, K)]
    a = mxq(f64(w1), 0, "e4m3").T @ xq
    z = f64(ga) * (a[:, unstriped(n1)] - a[:, unstriped(n2)])
    x_two = unpack_weight(x_words, x_scales)[:, unstriped(two)]
    b = mxq(f64(w2), 0, "e4m3").T @ x_two
    z2 = f64(gb) * (relu(b - b[:, unstriped(n3)]) + 0.5 * (relu(b[:, unstriped(n4)] - b)))
    s = 0.0625 * ((mxq(z, 0, "e4m3").T @ mxq(z2, 0, "e4m3")))
    ex = np.exp(s)
    return np.log(ex + ex[:, unstriped(n5)]) - s[:, unstriped(n6)]

@@ -1,0 +1,241 @@
+from contextlib import ExitStack
+
+import concourse.mybir as mybir
+
+F32 = mybir.dt.float32
+BF16 = mybir.dt.bfloat16
+I32 = mybir.dt.int32
+U32 = mybir.dt.uint32
+U16 = mybir.dt.uint16
+U8 = mybir.dt.uint8
+FP8X4 = mybir.dt.float8_e4m3fn_x4
+ALU = mybir.AluOpType
+ACT = mybir.ActivationFunctionType
+
+P = 128
+PACK = 4
+T = 2048
+N = 512
+HALF = N // 2
+LIST_HALF = HALF // 16
+QUADS = 4
+
+FLOPS = 3 * 2 * 512 * 512 * 512
+
+
+def tile_picked_hkqgaphingelse_none_p_kernel(
+    tc, x_words, x_scales, w1, w2, ga, gb, offs, two, n1, n2, n3, n4, n5, n6, out
+):
+    nc = tc.nc
+    with ExitStack() as ctx:
+        lists = ctx.enter_context(tc.tile_pool(name="lists", bufs=1))
+        sb = ctx.enter_context(tc.tile_pool(name="sb", bufs=1))
+        psum = ctx.enter_context(tc.psum_pool(name="psum", bufs=1))
+
+        def load_list(src, name):
+            tile = lists.tile([P, N // 16], U16, name=name)
+            nc.sync.dma_start(tile[:], src)
+            return tile
+
+        def list_half(tile, h):
+            return tile[:, h * LIST_HALF : (h + 1) * LIST_HALF]
+
+        def cols(h):
+            return slice(h * HALF, (h + 1) * HALF)
+
+        def load_weight_half(w, h, name):
+            raw = sb.tile([P, PACK, HALF], F32, name=name)
+            nc.sync.dma_start(raw[:], w.rearrange("(p j) c -> p j c", j=PACK)[:, :, cols(h)])
+            return raw
+
+        def load_gain(g, name):
+            tile = sb.tile([P, PACK], F32, name=name)
+            nc.sync.dma_start(tile[:], g.rearrange("(p t) o -> p (t o)", t=PACK))
+            return tile
+
+        scales_two = sb.tile([P, T], U8, name="scales_two", align_bytes=64)
+        nc.gpsimd.memset(scales_two[:].bitcast(I32), 0)
+        scales_offs = sb.tile([P, T], U8, name="scales_offs", align_bytes=64)
+        nc.gpsimd.memset(scales_offs[:].bitcast(I32), 0)
+        xa_scale = sb.tile([P, N], U8, name="xa_scale", align_bytes=64)
+        nc.gpsimd.memset(xa_scale[:].bitcast(I32), 0)
+        for q in range(QUADS):
+            rows = x_scales[0, 4 * q : 4 * q + 4, :].bitcast(I32)
+            nc.scalar.dma_start(scales_two[32 * q : 32 * q + 4, :].bitcast(I32), rows)
+        nc.scalar.dma_start(scales_offs[0:P:8, :].bitcast(I32), x_scales[0].bitcast(I32))
+
+        gb_t = load_gain(gb, "gb_t")
+        two_t = load_list(two, "two_t")
+        w2_raw = [load_weight_half(w2, h, "w2_raw%d" % h) for h in range(2)]
+        words = sb.tile([P, T], I32, name="words", align_bytes=64)
+        nc.sync.dma_start(words[:], x_words[0].rearrange("p n t -> p (n t)").bitcast(I32))
+        offs_t = load_list(offs, "offs_t")
+        w1_raw = [load_weight_half(w1, h, "w1_raw%d" % h) for h in range(2)]
+        n3_t = load_list(n3, "n3_t")
+        n4_t = load_list(n4, "n4_t")
+        ga_t = load_gain(ga, "ga_t")
+        n1_t = load_list(n1, "n1_t")
+        n2_t = load_list(n2, "n2_t")
+        n5_t = load_list(n5, "n5_t")
+        n6_t = load_list(n6, "n6_t")
+
+        gb_neg = sb.tile([P, PACK], F32, name="gb_neg")
+        nc.scalar.activation(gb_neg[:], gb_t[:], ACT.Copy, scale=-1.0)
+        gb_half = sb.tile([P, PACK], F32, name="gb_half")
+        nc.scalar.activation(gb_half[:], gb_t[:], ACT.Copy, scale=0.5)
+
+        def round_weight(raw, name):
+            dealt = sb.tile([P, PACK, P, PACK], BF16, name=name, align_bytes=64)
+            for h in range(2):
+                nc.scalar.activation(
+                    dealt[:, :, h * (P // 2) : (h + 1) * (P // 2), :].rearrange("p t m j -> p m j t"),
+                    raw[h][:].rearrange("p j (m t) -> p m j t", t=PACK),
+                    ACT.Copy,
+                )
+            return dealt
+
+        def quantize_weight(dealt, name):
+            codes = sb.tile([P, N], U32, name=name + "_codes", align_bytes=64)
+            scale = sb.tile([P, N], U8, name=name + "_scale", align_bytes=64)
+            for t in range(PACK):
+                nc.vector.quantize_mx(
+                    out=codes[:, t * P : (t + 1) * P].bitcast(FP8X4),
+                    scales=scale[:, t * P : (t + 1) * P],
+                    in_=dealt[:, t, :, :].rearrange("p m j -> p (m j)"),
+                )
+            return codes, scale
+
+        def product(bank, lhs_codes, lhs_scale, rhs_codes, rhs_scale):
+            nc.tensor.matmul_mx(
+                out=bank,
+                lhsT=lhs_codes.bitcast(FP8X4),
+                lhsT_scale=lhs_scale,
+                rhs=rhs_codes.bitcast(FP8X4),
+                rhs_scale=rhs_scale,
+                start=True,
+                stop=True,
+            )
+
+        def interleave(dst, h, in0, in1, op):
+            nc.vector.tensor_tensor(
+                dst.rearrange("p (c i t) -> p c t i", i=4, t=PACK),
+                in0.rearrange("p t (c i) -> p c t i", i=4),
+                in1.rearrange("p t (c i) -> p c t i", i=4),
+                op,
+            )
+
+        xb_scale = sb.tile([P, N], U8, name="xb_scale", align_bytes=64)
+        nc.vector.tensor_copy(xb_scale[:], scales_two[:].indirect(two_t[:]))
+        w2_dealt = round_weight(w2_raw, "w2_dealt")
+        xa_picked = sb.tile([P, N], U8, name="xa_picked", align_bytes=64)
+        nc.vector.tensor_copy(xa_picked[:], scales_offs[:].indirect(offs_t[:]))
+        for r in range(4):
+            nc.sync.dma_start(xa_scale[r:P:32, :].bitcast(I32), xa_picked[8 * r : P : 32, :].bitcast(I32))
+        w2_codes, w2_scale = quantize_weight(w2_dealt, "w2")
+        xb_codes = sb.tile([P, N], U32, name="xb_codes", align_bytes=64)
+        nc.vector.tensor_copy(xb_codes[:], words[:].bitcast(U32).indirect(two_t[:]))
+        xa_codes = sb.tile([P, N], U32, name="xa_codes", align_bytes=64)
+        nc.vector.tensor_copy(xa_codes[:], words[:].bitcast(U32).indirect(offs_t[:]))
+
+        b_win, b_plain = [], []
+        b_bank = []
+        for t in range(PACK):
+            bank = psum.tile([P, N], F32, name="bank%d" % t)
+            tc_cols = slice(t * P, (t + 1) * P)
+            product(bank[:], w2_codes[:, tc_cols], w2_scale[:, tc_cols], xb_codes[:], xb_scale[:])
+            b_bank.append(bank)
+        for t in range(PACK):
+            win = sb.tile([P, N], F32, name="b_win%d" % t)
+            plain = sb.tile([P, N], F32, name="b_plain%d" % t)
+            nc.scalar.activation(win[:], b_bank[t][:], ACT.Copy)
+            nc.scalar.activation(plain[:], b_bank[t][:], ACT.Copy)
+            b_win.append(win)
+            b_plain.append(plain)
+            if t == 0:
+                w1_dealt = round_weight(w1_raw, "w1_dealt")
+
+        d3 = sb.tile([P, PACK, N], F32, name="d3")
+        d4 = sb.tile([P, PACK, N], F32, name="d4")
+        r3 = sb.tile([P, PACK, N], F32, name="r3")
+        r4 = sb.tile([P, PACK, N], F32, name="r4")
+
+        def hinge_gathers(t):
+            for h in range(2):
+                nc.vector.tensor_tensor(
+                    d3[:, t, cols(h)], b_win[t][:].indirect(list_half(n3_t, h)), b_plain[t][:, cols(h)], ALU.subtract
+                )
+            for h in range(2):
+                nc.vector.tensor_tensor(
+                    d4[:, t, cols(h)], b_win[t][:].indirect(list_half(n4_t, h)), b_plain[t][:, cols(h)], ALU.subtract
+                )
+
+        def hinge_parts(t):
+            nc.vector.tensor_scalar(r3[:, t, :], d3[:, t, :], 0.0, gb_neg[:, t : t + 1], ALU.min, ALU.mult)
+            nc.vector.tensor_scalar(r4[:, t, :], d4[:, t, :], 0.0, gb_half[:, t : t + 1], ALU.max, ALU.mult)
+
+        hinge_gathers(0)
+        w1_codes, w1_scale = quantize_weight(w1_dealt, "w1")
+
+        a_win = []
+        for t in range(PACK):
+            bank = psum.tile([P, N], F32, name="bank%d" % (PACK + t))
+            tc_cols = slice(t * P, (t + 1) * P)
+            product(bank[:], w1_codes[:, tc_cols], w1_scale[:, tc_cols], xa_codes[:], xa_scale[:])
+            win = sb.tile([P, N], F32, name="a_win%d" % t)
+            nc.scalar.activation(win[:], bank[:], ACT.Copy, scale=ga_t[:, t : t + 1])
+            a_win.append(win)
+        g1 = [sb.tile([P, PACK, HALF], F32, name="g1_%d" % h) for h in range(2)]
+        g2 = [sb.tile([P, PACK, HALF], F32, name="g2_%d" % h) for h in range(2)]
+        for h in range(2):
+            for t in range(PACK):
+                nc.scalar.activation(g1[h][:, t, :], a_win[t][:].indirect(list_half(n1_t, h)), ACT.Copy)
+                nc.scalar.activation(g2[h][:, t, :], a_win[t][:].indirect(list_half(n2_t, h)), ACT.Copy)
+
+        for t in range(1, PACK):
+            hinge_gathers(t)
+            hinge_parts(t - 1)
+        hinge_parts(PACK - 1)
+
+        z2_codes = sb.tile([P, N], U32, name="z2_codes", align_bytes=64)
+        z2_scale = sb.tile([P, N], U8, name="z2_scale", align_bytes=64)
+        z2_bf = [sb.tile([P, HALF * PACK], BF16, name="z2_bf%d" % h, align_bytes=64) for h in range(2)]
+        z_bf = [sb.tile([P, HALF * PACK], BF16, name="z_bf%d" % h, align_bytes=64) for h in range(2)]
+        z_codes = [sb.tile([P, HALF], U32, name="z_codes%d" % h, align_bytes=64) for h in range(2)]
+        z_scale = [sb.tile([P, HALF], U8, name="z_scale%d" % h, align_bytes=64) for h in range(2)]
+        for h in range(2):
+            interleave(z2_bf[h][:], h, r3[:, :, cols(h)], r4[:, :, cols(h)], ALU.add)
+        interleave(z_bf[0][:], 0, g1[0][:], g2[0][:], ALU.subtract)
+        for h in range(2):
+            nc.vector.quantize_mx(out=z2_codes[:, cols(h)].bitcast(FP8X4), scales=z2_scale[:, cols(h)], in_=z2_bf[h][:])
+        nc.vector.quantize_mx(out=z_codes[0][:].bitcast(FP8X4), scales=z_scale[0][:], in_=z_bf[0][:])
+        interleave(z_bf[1][:], 1, g1[1][:], g2[1][:], ALU.subtract)
+        nc.vector.quantize_mx(out=z_codes[1][:].bitcast(FP8X4), scales=z_scale[1][:], in_=z_bf[1][:])
+
+        pair = sb.tile([P, 4, N], F32, name="pair")
+        s_neg = []
+        ex = []
+        for i in range(4):
+            bank = psum.tile([P, N], F32, name="bank%d" % i)
+            rows = slice((i % 2) * P, (i % 2 + 1) * P)
+            product(bank[:], z_codes[i // 2][:, rows], z_scale[i // 2][:, rows], z2_codes[:], z2_scale[:])
+            ex_i = sb.tile([P, N], F32, name="ex%d" % i)
+            neg_i = sb.tile([P, N], F32, name="s_neg%d" % i)
+            nc.scalar.activation(ex_i[:], bank[:], ACT.Exp, scale=0.0625)
+            nc.vector.tensor_scalar(neg_i[:], bank[:], -0.0625, None, ALU.mult)
+            ex.append(ex_i)
+            s_neg.append(neg_i)
+        for i in (0, 2, 1, 3):
+            ex5 = sb.tile([P, N], F32, name="ex5_%d" % i)
+            for h in range(2):
+                nc.scalar.activation(ex5[:, cols(h)], ex[i][:].indirect(list_half(n5_t, h)), ACT.Copy)
+            nc.vector.tensor_tensor(pair[:, i, :], ex[i][:], ex5[:], ALU.add)
+        logs = sb.tile([P, 4, N], F32, name="logs")
+        for first in range(2):
+            for h in range(2):
+                nc.scalar.activation(logs[:, first::2, cols(h)], pair[:, first::2, cols(h)], ACT.Ln)
+                for i in (first, first + 2):
+                    res = sb.tile([P, HALF], F32, name="res%d_%d" % (i, h))
+                    nc.vector.tensor_tensor(
+                        res[:], s_neg[i][:].indirect(list_half(n6_t, h)), logs[:, i, cols(h)], ALU.add
+                    )
+                    nc.sync.dma_start(out[i * P : (i + 1) * P, cols(h)], res[:])

@@ -18,6 +18,13 @@ T = 2048
 N = 512
 HALF = N // 2
 LIST_HALF = HALF // 16
+SPARE = 16
+LAST = 3
+PLAIN_BY = "VSDD"
+N4_ON_SCALAR = [3]
+NEG_ON_SCALAR = [0]
+N5_ON_VECTOR = [1]
+N6_ON_SCALAR = []
 QUADS = 4
 
 FLOPS = 3 * 2 * 512 * 512 * 512
@@ -48,9 +55,9 @@ def tile_picked_hkqgaphingelse_none_p_kernel(
             nc.sync.dma_start(raw[:], w.rearrange("(p j) c -> p j c", j=PACK)[:, :, cols(h)])
             return raw
 
-        def load_gain(g, name):
+        def load_gain(queue, g, name):
             tile = sb.tile([P, PACK], F32, name=name)
-            nc.sync.dma_start(tile[:], g.rearrange("(p t) o -> p (t o)", t=PACK))
+            queue.dma_start(tile[:], g.rearrange("(p t) o -> p (t o)", t=PACK))
             return tile
 
         scales_two = sb.tile([P, T], U8, name="scales_two", align_bytes=64)
@@ -64,25 +71,29 @@ def tile_picked_hkqgaphingelse_none_p_kernel(
             nc.scalar.dma_start(scales_two[32 * q : 32 * q + 4, :].bitcast(I32), rows)
         nc.scalar.dma_start(scales_offs[0:P:8, :].bitcast(I32), x_scales[0].bitcast(I32))
 
-        gb_t = load_gain(gb, "gb_t")
         two_t = load_list(two, "two_t")
+        offs_t = load_list(offs, "offs_t")
         w2_raw = [load_weight_half(w2, h, "w2_raw%d" % h) for h in range(2)]
         words = sb.tile([P, T], I32, name="words", align_bytes=64)
         nc.sync.dma_start(words[:], x_words[0].rearrange("p n t -> p (n t)").bitcast(I32))
-        offs_t = load_list(offs, "offs_t")
         w1_raw = [load_weight_half(w1, h, "w1_raw%d" % h) for h in range(2)]
         n3_t = load_list(n3, "n3_t")
         n4_t = load_list(n4, "n4_t")
-        ga_t = load_gain(ga, "ga_t")
+        gb_t = load_gain(nc.sync, gb, "gb_t")
+        ga_t = load_gain(nc.sync, ga, "ga_t")
         n1_t = load_list(n1, "n1_t")
         n2_t = load_list(n2, "n2_t")
         n5_t = load_list(n5, "n5_t")
         n6_t = load_list(n6, "n6_t")
 
-        gb_neg = sb.tile([P, PACK], F32, name="gb_neg")
-        nc.scalar.activation(gb_neg[:], gb_t[:], ACT.Copy, scale=-1.0)
-        gb_half = sb.tile([P, PACK], F32, name="gb_half")
-        nc.scalar.activation(gb_half[:], gb_t[:], ACT.Copy, scale=0.5)
+        def window(name, spare):
+            tile = sb.tile([P, N + spare], F32, name=name)
+            nc.gpsimd.memset(tile[:, N:], 0.0)
+            return tile
+
+        b_win = [window("b_win%d" % t, N) for t in range(PACK)]
+        ex = [window("ex%d" % i, SPARE) for i in range(4)]
+        s_neg = [window("s_neg%d" % i, SPARE) for i in range(4)]
 
         def round_weight(raw, name):
             dealt = sb.tile([P, PACK, P, PACK], BF16, name=name, align_bytes=64)
@@ -116,7 +127,7 @@ def tile_picked_hkqgaphingelse_none_p_kernel(
                 stop=True,
             )
 
-        def interleave(dst, h, in0, in1, op):
+        def interleave(dst, in0, in1, op):
             nc.vector.tensor_tensor(
                 dst.rearrange("p (c i t) -> p c t i", i=4, t=PACK),
                 in0.rearrange("p t (c i) -> p c t i", i=4),
@@ -127,6 +138,9 @@ def tile_picked_hkqgaphingelse_none_p_kernel(
         xb_scale = sb.tile([P, N], U8, name="xb_scale", align_bytes=64)
         nc.vector.tensor_copy(xb_scale[:], scales_two[:].indirect(two_t[:]))
         w2_dealt = round_weight(w2_raw, "w2_dealt")
+        gb_half = sb.tile([P, PACK], F32, name="gb_half")
+        nc.gpsimd.tensor_scalar(gb_half[:], gb_t[:], 0.5, 0.0, ALU.mult, ALU.add)
+
         xa_picked = sb.tile([P, N], U8, name="xa_picked", align_bytes=64)
         nc.vector.tensor_copy(xa_picked[:], scales_offs[:].indirect(offs_t[:]))
         for r in range(4):
@@ -137,7 +151,7 @@ def tile_picked_hkqgaphingelse_none_p_kernel(
         xa_codes = sb.tile([P, N], U32, name="xa_codes", align_bytes=64)
         nc.vector.tensor_copy(xa_codes[:], words[:].bitcast(U32).indirect(offs_t[:]))
 
-        b_win, b_plain = [], []
+        b_plain = []
         b_bank = []
         for t in range(PACK):
             bank = psum.tile([P, N], F32, name="bank%d" % t)
@@ -145,11 +159,14 @@ def tile_picked_hkqgaphingelse_none_p_kernel(
             product(bank[:], w2_codes[:, tc_cols], w2_scale[:, tc_cols], xb_codes[:], xb_scale[:])
             b_bank.append(bank)
         for t in range(PACK):
-            win = sb.tile([P, N], F32, name="b_win%d" % t)
             plain = sb.tile([P, N], F32, name="b_plain%d" % t)
-            nc.scalar.activation(win[:], b_bank[t][:], ACT.Copy)
-            nc.scalar.activation(plain[:], b_bank[t][:], ACT.Copy)
-            b_win.append(win)
+            nc.scalar.copy(b_win[t][:, :N], b_bank[t][:])
+            if PLAIN_BY[t] == "S":
+                nc.scalar.copy(plain[:], b_bank[t][:])
+            elif PLAIN_BY[t] == "V":
+                nc.vector.tensor_copy(plain[:], b_win[t][:, :N])
+            else:
+                nc.sync.dma_start(plain[:], b_win[t][:, :N])
             b_plain.append(plain)
             if t == 0:
                 w1_dealt = round_weight(w1_raw, "w1_dealt")
@@ -158,19 +175,21 @@ def tile_picked_hkqgaphingelse_none_p_kernel(
         d4 = sb.tile([P, PACK, N], F32, name="d4")
         r3 = sb.tile([P, PACK, N], F32, name="r3")
         r4 = sb.tile([P, PACK, N], F32, name="r4")
+        b4 = {}
+
+        def fetch_b4(t):
+            b4[t] = sb.tile([P, N], F32, name="b4_%d" % t)
+            nc.scalar.activation(b4[t][:], b_win[t][:].indirect(n4_t[:]), ACT.Copy)
 
         def hinge_gathers(t):
-            for h in range(2):
-                nc.vector.tensor_tensor(
-                    d3[:, t, cols(h)], b_win[t][:].indirect(list_half(n3_t, h)), b_plain[t][:, cols(h)], ALU.subtract
-                )
-            for h in range(2):
-                nc.vector.tensor_tensor(
-                    d4[:, t, cols(h)], b_win[t][:].indirect(list_half(n4_t, h)), b_plain[t][:, cols(h)], ALU.subtract
-                )
+            nc.vector.tensor_tensor(d3[:, t, :], b_win[t][:].indirect(n3_t[:]), b_plain[t][:], ALU.subtract)
+            if t in N4_ON_SCALAR:
+                nc.vector.tensor_tensor(d4[:, t, :], b4[t][:], b_plain[t][:], ALU.subtract)
+            else:
+                nc.vector.tensor_tensor(d4[:, t, :], b_win[t][:].indirect(n4_t[:]), b_plain[t][:], ALU.subtract)
 
         def hinge_parts(t):
-            nc.vector.tensor_scalar(r3[:, t, :], d3[:, t, :], 0.0, gb_neg[:, t : t + 1], ALU.min, ALU.mult)
+            nc.vector.tensor_scalar(r3[:, t, :], d3[:, t, :], 0.0, gb_t[:, t : t + 1], ALU.min, ALU.mult)
             nc.vector.tensor_scalar(r4[:, t, :], d4[:, t, :], 0.0, gb_half[:, t : t + 1], ALU.max, ALU.mult)
 
         hinge_gathers(0)
@@ -184,6 +203,8 @@ def tile_picked_hkqgaphingelse_none_p_kernel(
             win = sb.tile([P, N], F32, name="a_win%d" % t)
             nc.scalar.activation(win[:], bank[:], ACT.Copy, scale=ga_t[:, t : t + 1])
             a_win.append(win)
+        for t in N4_ON_SCALAR:
+            fetch_b4(t)
         g1 = [sb.tile([P, PACK, HALF], F32, name="g1_%d" % h) for h in range(2)]
         g2 = [sb.tile([P, PACK, HALF], F32, name="g2_%d" % h) for h in range(2)]
         for h in range(2):
@@ -199,43 +220,81 @@ def tile_picked_hkqgaphingelse_none_p_kernel(
         z2_codes = sb.tile([P, N], U32, name="z2_codes", align_bytes=64)
         z2_scale = sb.tile([P, N], U8, name="z2_scale", align_bytes=64)
         z2_bf = [sb.tile([P, HALF * PACK], BF16, name="z2_bf%d" % h, align_bytes=64) for h in range(2)]
-        z_bf = [sb.tile([P, HALF * PACK], BF16, name="z_bf%d" % h, align_bytes=64) for h in range(2)]
-        z_codes = [sb.tile([P, HALF], U32, name="z_codes%d" % h, align_bytes=64) for h in range(2)]
-        z_scale = [sb.tile([P, HALF], U8, name="z_scale%d" % h, align_bytes=64) for h in range(2)]
+        z_bf = [sb.tile([P, P * PACK], BF16, name="z_bf%d" % i, align_bytes=64) for i in range(4)]
+        z_codes = [sb.tile([P, P], U32, name="z_codes%d" % i, align_bytes=64) for i in range(4)]
+        z_scale = [sb.tile([P, P], U8, name="z_scale%d" % i, align_bytes=64) for i in range(4)]
+
+        def round_z(i):
+            rows = slice((i % 2) * P, (i % 2 + 1) * P)
+            interleave(z_bf[i][:], g1[i // 2][:, :, rows], g2[i // 2][:, :, rows], ALU.subtract)
+
+        def quantize_z(i):
+            nc.vector.quantize_mx(out=z_codes[i][:].bitcast(FP8X4), scales=z_scale[i][:], in_=z_bf[i][:])
+
         for h in range(2):
-            interleave(z2_bf[h][:], h, r3[:, :, cols(h)], r4[:, :, cols(h)], ALU.add)
-        interleave(z_bf[0][:], 0, g1[0][:], g2[0][:], ALU.subtract)
+            interleave(z2_bf[h][:], r4[:, :, cols(h)], r3[:, :, cols(h)], ALU.subtract)
+        round_z(0)
         for h in range(2):
             nc.vector.quantize_mx(out=z2_codes[:, cols(h)].bitcast(FP8X4), scales=z2_scale[:, cols(h)], in_=z2_bf[h][:])
-        nc.vector.quantize_mx(out=z_codes[0][:].bitcast(FP8X4), scales=z_scale[0][:], in_=z_bf[0][:])
-        interleave(z_bf[1][:], 1, g1[1][:], g2[1][:], ALU.subtract)
-        nc.vector.quantize_mx(out=z_codes[1][:].bitcast(FP8X4), scales=z_scale[1][:], in_=z_bf[1][:])
+        for i in range(1, 4):
+            quantize_z(i - 1)
+            round_z(i)
+        quantize_z(3)
 
-        pair = sb.tile([P, 4, N], F32, name="pair")
-        s_neg = []
-        ex = []
-        for i in range(4):
+        def scores(i):
             bank = psum.tile([P, N], F32, name="bank%d" % i)
-            rows = slice((i % 2) * P, (i % 2 + 1) * P)
-            product(bank[:], z_codes[i // 2][:, rows], z_scale[i // 2][:, rows], z2_codes[:], z2_scale[:])
-            ex_i = sb.tile([P, N], F32, name="ex%d" % i)
-            neg_i = sb.tile([P, N], F32, name="s_neg%d" % i)
-            nc.scalar.activation(ex_i[:], bank[:], ACT.Exp, scale=0.0625)
-            nc.vector.tensor_scalar(neg_i[:], bank[:], -0.0625, None, ALU.mult)
-            ex.append(ex_i)
-            s_neg.append(neg_i)
-        for i in (0, 2, 1, 3):
+            product(bank[:], z_codes[i][:], z_scale[i][:], z2_codes[:], z2_scale[:])
+            nc.scalar.activation(ex[i][:, :N], bank[:], ACT.Exp, scale=0.0625)
+            if i in NEG_ON_SCALAR:
+                nc.scalar.activation(s_neg[i][:, :N], bank[:], ACT.Copy, scale=-0.0625)
+            else:
+                nc.vector.tensor_scalar(s_neg[i][:, :N], bank[:], -0.0625, None, ALU.mult)
+
+        def fetch_ex5(i):
             ex5 = sb.tile([P, N], F32, name="ex5_%d" % i)
-            for h in range(2):
-                nc.scalar.activation(ex5[:, cols(h)], ex[i][:].indirect(list_half(n5_t, h)), ACT.Copy)
-            nc.vector.tensor_tensor(pair[:, i, :], ex[i][:], ex5[:], ALU.add)
-        logs = sb.tile([P, 4, N], F32, name="logs")
-        for first in range(2):
-            for h in range(2):
-                nc.scalar.activation(logs[:, first::2, cols(h)], pair[:, first::2, cols(h)], ACT.Ln)
-                for i in (first, first + 2):
-                    res = sb.tile([P, HALF], F32, name="res%d_%d" % (i, h))
+            nc.scalar.activation(ex5[:], ex[i][:].indirect(n5_t[:]), ACT.Copy)
+            return ex5
+
+        def take_log(i, pair):
+            logs = sb.tile([P, N], F32, name="z_codes3" if i == 0 else "logs%d" % i, align_bytes=64)
+            nc.scalar.activation(logs[:], pair, ACT.Ln)
+            return logs
+
+        def finish(i, logs):
+            res = sb.tile([P, N], F32, name="res%d" % i)
+            if i in N6_ON_SCALAR:
+                s6 = sb.tile([P, N], F32, name="s6_%d" % i)
+                nc.scalar.activation(s6[:], s_neg[i][:].indirect(n6_t[:]), ACT.Copy)
+                nc.vector.tensor_tensor(res[:], s6[:], logs[:], ALU.add)
+                nc.sync.dma_start(out[i * P : (i + 1) * P, :], res[:])
+            elif i != LAST:
+                nc.vector.tensor_tensor(res[:], s_neg[i][:].indirect(n6_t[:]), logs[:], ALU.add)
+                nc.sync.dma_start(out[i * P : (i + 1) * P, :], res[:])
+            else:
+                for h in range(2):
                     nc.vector.tensor_tensor(
-                        res[:], s_neg[i][:].indirect(list_half(n6_t, h)), logs[:, i, cols(h)], ALU.add
+                        res[:, cols(h)], s_neg[i][:].indirect(list_half(n6_t, h)), logs[:, cols(h)], ALU.add
                     )
-                    nc.sync.dma_start(out[i * P : (i + 1) * P, cols(h)], res[:])
+                    nc.sync.dma_start(out[i * P : (i + 1) * P, cols(h)], res[:, cols(h)])
+
+        def add_pair(i, pair, ex5):
+            if i in N5_ON_VECTOR:
+                twin = sb.tile([P, N], F32, name="ex_twin%d" % i)
+                nc.vector.tensor_copy(twin[:], ex[i][:, :N])
+                nc.vector.tensor_tensor(pair, ex[i][:].indirect(n5_t[:]), twin[:], ALU.add)
+            else:
+                nc.vector.tensor_tensor(pair, ex[i][:, :N], ex5[:], ALU.add)
+
+        scores(0)
+        scores(1)
+        ex5_0 = fetch_ex5(0)
+        scores(2)
+        scores(3)
+        pairs = [sb.tile([P, N], F32, name="pair%d" % i) for i in range(4)]
+        add_pair(0, pairs[0][:], ex5_0)
+        logs = [take_log(0, pairs[0][:])]
+        for i in range(1, 4):
+            add_pair(i, pairs[i][:], None if i in N5_ON_VECTOR else fetch_ex5(i))
+            finish(i - 1, logs[i - 1])
+            logs.append(take_log(i, pairs[i][:]))
+        finish(3, logs[3])

@@ -19,11 +19,13 @@ N = 512
 HALF = N // 2
 LIST_HALF = HALF // 16
 SPARE = 16
+LAG = 1
+EARLY = [0,3]
 LAST = 3
 PLAIN_BY = "VSDD"
 N4_ON_SCALAR = [3]
-NEG_ON_SCALAR = [0]
-N5_ON_VECTOR = [1]
+NEG_ON_SCALAR = []
+N5_ON_VECTOR = [1,2]
 N6_ON_SCALAR = []
 QUADS = 4
 
@@ -99,8 +101,8 @@ def tile_picked_hkqgaphingelse_none_p_kernel(
             dealt = sb.tile([P, PACK, P, PACK], BF16, name=name, align_bytes=64)
             for h in range(2):
                 nc.scalar.activation(
-                    dealt[:, :, h * (P // 2) : (h + 1) * (P // 2), :].rearrange("p t m j -> p m j t"),
-                    raw[h][:].rearrange("p j (m t) -> p m j t", t=PACK),
+                    dealt[:, :, h * (P // 2) : (h + 1) * (P // 2), :].rearrange("p t m j -> p m t j"),
+                    raw[h][:].rearrange("p j (m t) -> p m t j", t=PACK),
                     ACT.Copy,
                 )
             return dealt
@@ -192,9 +194,11 @@ def tile_picked_hkqgaphingelse_none_p_kernel(
             nc.vector.tensor_scalar(r3[:, t, :], d3[:, t, :], 0.0, gb_t[:, t : t + 1], ALU.min, ALU.mult)
             nc.vector.tensor_scalar(r4[:, t, :], d4[:, t, :], 0.0, gb_half[:, t : t + 1], ALU.max, ALU.mult)
 
-        hinge_gathers(0)
         w1_codes, w1_scale = quantize_weight(w1_dealt, "w1")
+        hinge_gathers(0)
 
+        for t in N4_ON_SCALAR:
+            fetch_b4(t)
         a_win = []
         for t in range(PACK):
             bank = psum.tile([P, N], F32, name="bank%d" % (PACK + t))
@@ -203,8 +207,6 @@ def tile_picked_hkqgaphingelse_none_p_kernel(
             win = sb.tile([P, N], F32, name="a_win%d" % t)
             nc.scalar.activation(win[:], bank[:], ACT.Copy, scale=ga_t[:, t : t + 1])
             a_win.append(win)
-        for t in N4_ON_SCALAR:
-            fetch_b4(t)
         g1 = [sb.tile([P, PACK, HALF], F32, name="g1_%d" % h) for h in range(2)]
         g2 = [sb.tile([P, PACK, HALF], F32, name="g2_%d" % h) for h in range(2)]
         for h in range(2):
@@ -245,56 +247,54 @@ def tile_picked_hkqgaphingelse_none_p_kernel(
             bank = psum.tile([P, N], F32, name="bank%d" % i)
             product(bank[:], z_codes[i][:], z_scale[i][:], z2_codes[:], z2_scale[:])
             nc.scalar.activation(ex[i][:, :N], bank[:], ACT.Exp, scale=0.0625)
-            if i in NEG_ON_SCALAR:
-                nc.scalar.activation(s_neg[i][:, :N], bank[:], ACT.Copy, scale=-0.0625)
-            else:
-                nc.vector.tensor_scalar(s_neg[i][:, :N], bank[:], -0.0625, None, ALU.mult)
+            return bank
+
+        def inverse(i):
+            nc.scalar.activation(s_neg[i][:, :N], banks[i][:], ACT.Exp, scale=-0.0625)
 
         def fetch_ex5(i):
             ex5 = sb.tile([P, N], F32, name="ex5_%d" % i)
             nc.scalar.activation(ex5[:], ex[i][:].indirect(n5_t[:]), ACT.Copy)
             return ex5
 
-        def take_log(i, pair):
-            logs = sb.tile([P, N], F32, name="z_codes3" if i == 0 else "logs%d" % i, align_bytes=64)
-            nc.scalar.activation(logs[:], pair, ACT.Ln)
-            return logs
-
-        def finish(i, logs):
-            res = sb.tile([P, N], F32, name="res%d" % i)
-            if i in N6_ON_SCALAR:
-                s6 = sb.tile([P, N], F32, name="s6_%d" % i)
-                nc.scalar.activation(s6[:], s_neg[i][:].indirect(n6_t[:]), ACT.Copy)
-                nc.vector.tensor_tensor(res[:], s6[:], logs[:], ALU.add)
-                nc.sync.dma_start(out[i * P : (i + 1) * P, :], res[:])
-            elif i != LAST:
-                nc.vector.tensor_tensor(res[:], s_neg[i][:].indirect(n6_t[:]), logs[:], ALU.add)
-                nc.sync.dma_start(out[i * P : (i + 1) * P, :], res[:])
-            else:
-                for h in range(2):
-                    nc.vector.tensor_tensor(
-                        res[:, cols(h)], s_neg[i][:].indirect(list_half(n6_t, h)), logs[:, cols(h)], ALU.add
-                    )
-                    nc.sync.dma_start(out[i * P : (i + 1) * P, cols(h)], res[:, cols(h)])
-
-        def add_pair(i, pair, ex5):
+        def add_pair(i, ex5):
+            pair = sb.tile([P, N], F32, name="pair%d" % i)
             if i in N5_ON_VECTOR:
                 twin = sb.tile([P, N], F32, name="ex_twin%d" % i)
                 nc.vector.tensor_copy(twin[:], ex[i][:, :N])
-                nc.vector.tensor_tensor(pair, ex[i][:].indirect(n5_t[:]), twin[:], ALU.add)
+                nc.vector.tensor_tensor(pair[:], ex[i][:].indirect(n5_t[:]), twin[:], ALU.add)
             else:
-                nc.vector.tensor_tensor(pair, ex[i][:, :N], ex5[:], ALU.add)
+                nc.vector.tensor_tensor(pair[:], ex[i][:, :N], ex5[:], ALU.add)
+            return pair
 
-        scores(0)
-        scores(1)
-        ex5_0 = fetch_ex5(0)
-        scores(2)
-        scores(3)
-        pairs = [sb.tile([P, N], F32, name="pair%d" % i) for i in range(4)]
-        add_pair(0, pairs[0][:], ex5_0)
-        logs = [take_log(0, pairs[0][:])]
-        for i in range(1, 4):
-            add_pair(i, pairs[i][:], None if i in N5_ON_VECTOR else fetch_ex5(i))
-            finish(i - 1, logs[i - 1])
-            logs.append(take_log(i, pairs[i][:]))
-        finish(3, logs[3])
+        def divide(i, pair):
+            ratio = sb.tile([P, N], F32, name="ratio%d" % i)
+            pieces = 2 if i == 3 else 1
+            for h in range(pieces):
+                c = slice(h * N // pieces, (h + 1) * N // pieces)
+                entries = n6_t[:, c.start // 16 : c.stop // 16]
+                nc.vector.tensor_tensor(ratio[:, c], s_neg[i][:].indirect(entries), pair[:, c], ALU.mult)
+            return ratio
+
+        def finish(i, ratio):
+            res = sb.tile([P, N], F32, name="z_codes3" if i == 0 else "res%d" % i, align_bytes=64)
+            pieces = 2 if i == 3 else 1
+            for h in range(pieces):
+                c = slice(h * N // pieces, (h + 1) * N // pieces)
+                nc.scalar.activation(res[:, c], ratio[:, c], ACT.Ln)
+                nc.sync.dma_start(out[i * P : (i + 1) * P, c], res[:, c])
+
+        ex5 = {}
+        banks = []
+        for i in range(4 + LAG):
+            if i < 4:
+                banks.append(scores(i))
+            if i in EARLY:
+                ex5[i] = fetch_ex5(i)
+            if i >= LAG:
+                inverse(i - LAG)
+        pairs = [add_pair(0, ex5.get(0))]
+        for i in range(4):
+            if i < 3:
+                pairs.append(add_pair(i + 1, ex5.get(i + 1)))
+            finish(i, divide(i, pairs[i]))

@@ -17,17 +17,18 @@ PACK = 4
 T = 2048
 N = 512
 HALF = N // 2
-LIST_HALF = HALF // 16
-SPARE = 16
-LAG = 1
-EARLY = [0,3]
-LAST = 3
-PLAIN_BY = "VSDD"
-N4_ON_SCALAR = [3]
-NEG_ON_SCALAR = []
-N5_ON_VECTOR = [1,2]
-N6_ON_SCALAR = []
+PER_COLUMN = 16
 QUADS = 4
+BLOCKS = N // P
+LAST = BLOCKS - 1
+RUN = 4
+SCORE_SCALE = 0.0625
+
+B_SPARE = N
+S_SPARE = PER_COLUMN
+
+N4_TILE_ON_SCALAR = PACK - 1
+N5_BLOCKS_ON_SCALAR = (0, LAST)
 
 FLOPS = 3 * 2 * 512 * 512 * 512
 
@@ -41,25 +42,25 @@ def tile_picked_hkqgaphingelse_none_p_kernel(
         sb = ctx.enter_context(tc.tile_pool(name="sb", bufs=1))
         psum = ctx.enter_context(tc.psum_pool(name="psum", bufs=1))
 
+        def half(h):
+            return slice(h * HALF, (h + 1) * HALF)
+
+        def entries(list_tile, columns):
+            return list_tile[:, columns.start // PER_COLUMN : columns.stop // PER_COLUMN]
+
         def load_list(src, name):
-            tile = lists.tile([P, N // 16], U16, name=name)
+            tile = lists.tile([P, N // PER_COLUMN], U16, name=name)
             nc.sync.dma_start(tile[:], src)
             return tile
 
-        def list_half(tile, h):
-            return tile[:, h * LIST_HALF : (h + 1) * LIST_HALF]
-
-        def cols(h):
-            return slice(h * HALF, (h + 1) * HALF)
-
         def load_weight_half(w, h, name):
             raw = sb.tile([P, PACK, HALF], F32, name=name)
-            nc.sync.dma_start(raw[:], w.rearrange("(p j) c -> p j c", j=PACK)[:, :, cols(h)])
+            nc.sync.dma_start(raw[:], w.rearrange("(p j) c -> p j c", j=PACK)[:, :, half(h)])
             return raw
 
-        def load_gain(queue, g, name):
+        def load_gain(g, name):
             tile = sb.tile([P, PACK], F32, name=name)
-            queue.dma_start(tile[:], g.rearrange("(p t) o -> p (t o)", t=PACK))
+            nc.sync.dma_start(tile[:], g.rearrange("(p t) o -> p (t o)", t=PACK))
             return tile
 
         scales_two = sb.tile([P, T], U8, name="scales_two", align_bytes=64)
@@ -81,8 +82,8 @@ def tile_picked_hkqgaphingelse_none_p_kernel(
         w1_raw = [load_weight_half(w1, h, "w1_raw%d" % h) for h in range(2)]
         n3_t = load_list(n3, "n3_t")
         n4_t = load_list(n4, "n4_t")
-        gb_t = load_gain(nc.sync, gb, "gb_t")
-        ga_t = load_gain(nc.sync, ga, "ga_t")
+        gb_t = load_gain(gb, "gb_t")
+        ga_t = load_gain(ga, "ga_t")
         n1_t = load_list(n1, "n1_t")
         n2_t = load_list(n2, "n2_t")
         n5_t = load_list(n5, "n5_t")
@@ -93,19 +94,14 @@ def tile_picked_hkqgaphingelse_none_p_kernel(
             nc.gpsimd.memset(tile[:, N:], 0.0)
             return tile
 
-        b_win = [window("b_win%d" % t, N) for t in range(PACK)]
-        ex = [window("ex%d" % i, SPARE) for i in range(4)]
-        s_neg = [window("s_neg%d" % i, SPARE) for i in range(4)]
+        b_win = [window("b_win%d" % t, B_SPARE) for t in range(PACK)]
+        ex_win = [window("ex_win%d" % i, S_SPARE) for i in range(BLOCKS)]
+        inv_win = [window("inv_win%d" % i, S_SPARE) for i in range(BLOCKS)]
 
-        def round_weight(raw, name):
-            dealt = sb.tile([P, PACK, P, PACK], BF16, name=name, align_bytes=64)
-            for h in range(2):
-                nc.scalar.activation(
-                    dealt[:, :, h * (P // 2) : (h + 1) * (P // 2), :].rearrange("p t m j -> p m t j"),
-                    raw[h][:].rearrange("p j (m t) -> p m t j", t=PACK),
-                    ACT.Copy,
-                )
-            return dealt
+        def dealt_views(dealt, raw, h):
+            dst = dealt[:, :, h * (P // 2) : (h + 1) * (P // 2), :].rearrange("p t m j -> p m t j")
+            src = raw[h][:].rearrange("p j (m t) -> p m t j", t=PACK)
+            return dst, src
 
         def quantize_weight(dealt, name):
             codes = sb.tile([P, N], U32, name=name + "_codes", align_bytes=64)
@@ -118,9 +114,10 @@ def tile_picked_hkqgaphingelse_none_p_kernel(
                 )
             return codes, scale
 
-        def product(bank, lhs_codes, lhs_scale, rhs_codes, rhs_scale):
+        def product(bank_name, lhs_codes, lhs_scale, rhs_codes, rhs_scale):
+            bank = psum.tile([P, N], F32, name=bank_name)
             nc.tensor.matmul_mx(
-                out=bank,
+                out=bank[:],
                 lhsT=lhs_codes.bitcast(FP8X4),
                 lhsT_scale=lhs_scale,
                 rhs=rhs_codes.bitcast(FP8X4),
@@ -128,18 +125,22 @@ def tile_picked_hkqgaphingelse_none_p_kernel(
                 start=True,
                 stop=True,
             )
+            return bank
 
-        def interleave(dst, in0, in1, op):
+        def subtract_and_round(dst, in0, in1):
             nc.vector.tensor_tensor(
-                dst.rearrange("p (c i t) -> p c t i", i=4, t=PACK),
-                in0.rearrange("p t (c i) -> p c t i", i=4),
-                in1.rearrange("p t (c i) -> p c t i", i=4),
-                op,
+                dst.rearrange("p (r i t) -> p r t i", i=RUN, t=PACK),
+                in0.rearrange("p t (r i) -> p r t i", i=RUN),
+                in1.rearrange("p t (r i) -> p r t i", i=RUN),
+                ALU.subtract,
             )
 
         xb_scale = sb.tile([P, N], U8, name="xb_scale", align_bytes=64)
         nc.vector.tensor_copy(xb_scale[:], scales_two[:].indirect(two_t[:]))
-        w2_dealt = round_weight(w2_raw, "w2_dealt")
+        w2_dealt = sb.tile([P, PACK, P, PACK], BF16, name="w2_dealt", align_bytes=64)
+        w1_dealt = sb.tile([P, PACK, P, PACK], BF16, name="w1_dealt", align_bytes=64)
+        for h in range(2):
+            nc.scalar.activation(*dealt_views(w2_dealt, w2_raw, h), ACT.Copy)
         gb_half = sb.tile([P, PACK], F32, name="gb_half")
         nc.gpsimd.tensor_scalar(gb_half[:], gb_t[:], 0.5, 0.0, ALU.mult, ALU.add)
 
@@ -153,148 +154,125 @@ def tile_picked_hkqgaphingelse_none_p_kernel(
         xa_codes = sb.tile([P, N], U32, name="xa_codes", align_bytes=64)
         nc.vector.tensor_copy(xa_codes[:], words[:].bitcast(U32).indirect(offs_t[:]))
 
-        b_plain = []
-        b_bank = []
+        b_banks = []
         for t in range(PACK):
-            bank = psum.tile([P, N], F32, name="bank%d" % t)
-            tc_cols = slice(t * P, (t + 1) * P)
-            product(bank[:], w2_codes[:, tc_cols], w2_scale[:, tc_cols], xb_codes[:], xb_scale[:])
-            b_bank.append(bank)
+            tile_cols = slice(t * P, (t + 1) * P)
+            b_banks.append(
+                product("bank%d" % t, w2_codes[:, tile_cols], w2_scale[:, tile_cols], xb_codes[:], xb_scale[:])
+            )
+        nc.vector.tensor_copy(*dealt_views(w1_dealt, w1_raw, 0))
+        b_twin = []
         for t in range(PACK):
-            plain = sb.tile([P, N], F32, name="b_plain%d" % t)
-            nc.scalar.copy(b_win[t][:, :N], b_bank[t][:])
-            if PLAIN_BY[t] == "S":
-                nc.scalar.copy(plain[:], b_bank[t][:])
-            elif PLAIN_BY[t] == "V":
-                nc.vector.tensor_copy(plain[:], b_win[t][:, :N])
-            else:
-                nc.sync.dma_start(plain[:], b_win[t][:, :N])
-            b_plain.append(plain)
+            twin = sb.tile([P, N], F32, name="b_twin%d" % t)
+            nc.scalar.copy(b_win[t][:, :N], b_banks[t][:])
             if t == 0:
-                w1_dealt = round_weight(w1_raw, "w1_dealt")
+                nc.vector.tensor_copy(twin[:], b_win[t][:, :N])
+                nc.scalar.activation(*dealt_views(w1_dealt, w1_raw, 1), ACT.Copy)
+            else:
+                nc.sync.dma_start(twin[:], b_win[t][:, :N])
+            b_twin.append(twin)
 
         d3 = sb.tile([P, PACK, N], F32, name="d3")
         d4 = sb.tile([P, PACK, N], F32, name="d4")
-        r3 = sb.tile([P, PACK, N], F32, name="r3")
-        r4 = sb.tile([P, PACK, N], F32, name="r4")
-        b4 = {}
+        down = sb.tile([P, PACK, N], F32, name="down")
+        up = sb.tile([P, PACK, N], F32, name="up")
+        b4 = sb.tile([P, N], F32, name="b4")
 
-        def fetch_b4(t):
-            b4[t] = sb.tile([P, N], F32, name="b4_%d" % t)
-            nc.scalar.activation(b4[t][:], b_win[t][:].indirect(n4_t[:]), ACT.Copy)
+        def differences(t):
+            nc.vector.tensor_tensor(d3[:, t, :], b_win[t][:].indirect(n3_t[:]), b_twin[t][:], ALU.subtract)
+            looked_up = b4[:] if t == N4_TILE_ON_SCALAR else b_win[t][:].indirect(n4_t[:])
+            nc.vector.tensor_tensor(d4[:, t, :], looked_up, b_twin[t][:], ALU.subtract)
 
-        def hinge_gathers(t):
-            nc.vector.tensor_tensor(d3[:, t, :], b_win[t][:].indirect(n3_t[:]), b_plain[t][:], ALU.subtract)
-            if t in N4_ON_SCALAR:
-                nc.vector.tensor_tensor(d4[:, t, :], b4[t][:], b_plain[t][:], ALU.subtract)
-            else:
-                nc.vector.tensor_tensor(d4[:, t, :], b_win[t][:].indirect(n4_t[:]), b_plain[t][:], ALU.subtract)
-
-        def hinge_parts(t):
-            nc.vector.tensor_scalar(r3[:, t, :], d3[:, t, :], 0.0, gb_t[:, t : t + 1], ALU.min, ALU.mult)
-            nc.vector.tensor_scalar(r4[:, t, :], d4[:, t, :], 0.0, gb_half[:, t : t + 1], ALU.max, ALU.mult)
+        def hinges(t):
+            nc.vector.tensor_scalar(down[:, t, :], d3[:, t, :], 0.0, gb_t[:, t : t + 1], ALU.min, ALU.mult)
+            nc.vector.tensor_scalar(up[:, t, :], d4[:, t, :], 0.0, gb_half[:, t : t + 1], ALU.max, ALU.mult)
 
         w1_codes, w1_scale = quantize_weight(w1_dealt, "w1")
-        hinge_gathers(0)
+        differences(0)
+        nc.scalar.activation(b4[:], b_win[N4_TILE_ON_SCALAR][:].indirect(n4_t[:]), ACT.Copy)
 
-        for t in N4_ON_SCALAR:
-            fetch_b4(t)
         a_win = []
         for t in range(PACK):
-            bank = psum.tile([P, N], F32, name="bank%d" % (PACK + t))
-            tc_cols = slice(t * P, (t + 1) * P)
-            product(bank[:], w1_codes[:, tc_cols], w1_scale[:, tc_cols], xa_codes[:], xa_scale[:])
-            win = sb.tile([P, N], F32, name="a_win%d" % t)
-            nc.scalar.activation(win[:], bank[:], ACT.Copy, scale=ga_t[:, t : t + 1])
-            a_win.append(win)
-        g1 = [sb.tile([P, PACK, HALF], F32, name="g1_%d" % h) for h in range(2)]
-        g2 = [sb.tile([P, PACK, HALF], F32, name="g2_%d" % h) for h in range(2)]
+            tile_cols = slice(t * P, (t + 1) * P)
+            bank = product(
+                "bank%d" % (PACK + t), w1_codes[:, tile_cols], w1_scale[:, tile_cols], xa_codes[:], xa_scale[:]
+            )
+            weighted = sb.tile([P, N], F32, name="a_win%d" % t)
+            nc.scalar.activation(weighted[:], bank[:], ACT.Copy, scale=ga_t[:, t : t + 1])
+            a_win.append(weighted)
+        a1 = [sb.tile([P, PACK, HALF], F32, name="a1_%d" % h) for h in range(2)]
+        a2 = [sb.tile([P, PACK, HALF], F32, name="a2_%d" % h) for h in range(2)]
         for h in range(2):
             for t in range(PACK):
-                nc.scalar.activation(g1[h][:, t, :], a_win[t][:].indirect(list_half(n1_t, h)), ACT.Copy)
-                nc.scalar.activation(g2[h][:, t, :], a_win[t][:].indirect(list_half(n2_t, h)), ACT.Copy)
+                nc.scalar.activation(a1[h][:, t, :], a_win[t][:].indirect(entries(n1_t, half(h))), ACT.Copy)
+                nc.scalar.activation(a2[h][:, t, :], a_win[t][:].indirect(entries(n2_t, half(h))), ACT.Copy)
 
         for t in range(1, PACK):
-            hinge_gathers(t)
-            hinge_parts(t - 1)
-        hinge_parts(PACK - 1)
+            differences(t)
+            hinges(t - 1)
+        hinges(PACK - 1)
 
         z2_codes = sb.tile([P, N], U32, name="z2_codes", align_bytes=64)
         z2_scale = sb.tile([P, N], U8, name="z2_scale", align_bytes=64)
         z2_bf = [sb.tile([P, HALF * PACK], BF16, name="z2_bf%d" % h, align_bytes=64) for h in range(2)]
-        z_bf = [sb.tile([P, P * PACK], BF16, name="z_bf%d" % i, align_bytes=64) for i in range(4)]
-        z_codes = [sb.tile([P, P], U32, name="z_codes%d" % i, align_bytes=64) for i in range(4)]
-        z_scale = [sb.tile([P, P], U8, name="z_scale%d" % i, align_bytes=64) for i in range(4)]
+        z_bf = [sb.tile([P, P * PACK], BF16, name="z_bf%d" % i, align_bytes=64) for i in range(BLOCKS)]
+        z_codes = [sb.tile([P, P], U32, name="z_codes%d" % i, align_bytes=64) for i in range(BLOCKS)]
+        z_scale = [sb.tile([P, P], U8, name="z_scale%d" % i, align_bytes=64) for i in range(BLOCKS)]
 
         def round_z(i):
-            rows = slice((i % 2) * P, (i % 2 + 1) * P)
-            interleave(z_bf[i][:], g1[i // 2][:, :, rows], g2[i // 2][:, :, rows], ALU.subtract)
+            h, within = divmod(i * P, HALF)
+            columns = slice(within, within + P)
+            subtract_and_round(z_bf[i][:], a1[h][:, :, columns], a2[h][:, :, columns])
 
         def quantize_z(i):
             nc.vector.quantize_mx(out=z_codes[i][:].bitcast(FP8X4), scales=z_scale[i][:], in_=z_bf[i][:])
 
         for h in range(2):
-            interleave(z2_bf[h][:], r4[:, :, cols(h)], r3[:, :, cols(h)], ALU.subtract)
+            subtract_and_round(z2_bf[h][:], up[:, :, half(h)], down[:, :, half(h)])
         round_z(0)
         for h in range(2):
-            nc.vector.quantize_mx(out=z2_codes[:, cols(h)].bitcast(FP8X4), scales=z2_scale[:, cols(h)], in_=z2_bf[h][:])
-        for i in range(1, 4):
+            nc.vector.quantize_mx(out=z2_codes[:, half(h)].bitcast(FP8X4), scales=z2_scale[:, half(h)], in_=z2_bf[h][:])
+        for i in range(1, BLOCKS):
             quantize_z(i - 1)
             round_z(i)
-        quantize_z(3)
+        quantize_z(LAST)
 
-        def scores(i):
-            bank = psum.tile([P, N], F32, name="bank%d" % i)
-            product(bank[:], z_codes[i][:], z_scale[i][:], z2_codes[:], z2_scale[:])
-            nc.scalar.activation(ex[i][:, :N], bank[:], ACT.Exp, scale=0.0625)
-            return bank
+        s_banks = []
+        ex5 = {}
+        for i in range(BLOCKS + 1):
+            if i < BLOCKS:
+                s_banks.append(product("bank%d" % i, z_codes[i][:], z_scale[i][:], z2_codes[:], z2_scale[:]))
+                nc.scalar.activation(ex_win[i][:, :N], s_banks[i][:], ACT.Exp, scale=SCORE_SCALE)
+            if i in N5_BLOCKS_ON_SCALAR:
+                ex5[i] = sb.tile([P, N], F32, name="ex5_%d" % i)
+                nc.scalar.activation(ex5[i][:], ex_win[i][:].indirect(n5_t[:]), ACT.Copy)
+            if i >= 1:
+                nc.scalar.activation(inv_win[i - 1][:, :N], s_banks[i - 1][:], ACT.Exp, scale=-SCORE_SCALE)
 
-        def inverse(i):
-            nc.scalar.activation(s_neg[i][:, :N], banks[i][:], ACT.Exp, scale=-0.0625)
-
-        def fetch_ex5(i):
-            ex5 = sb.tile([P, N], F32, name="ex5_%d" % i)
-            nc.scalar.activation(ex5[:], ex[i][:].indirect(n5_t[:]), ACT.Copy)
-            return ex5
-
-        def add_pair(i, ex5):
+        def add_pair(i):
             pair = sb.tile([P, N], F32, name="pair%d" % i)
-            if i in N5_ON_VECTOR:
-                twin = sb.tile([P, N], F32, name="ex_twin%d" % i)
-                nc.vector.tensor_copy(twin[:], ex[i][:, :N])
-                nc.vector.tensor_tensor(pair[:], ex[i][:].indirect(n5_t[:]), twin[:], ALU.add)
+            if i in N5_BLOCKS_ON_SCALAR:
+                nc.vector.tensor_tensor(pair[:], ex_win[i][:, :N], ex5[i][:], ALU.add)
             else:
-                nc.vector.tensor_tensor(pair[:], ex[i][:, :N], ex5[:], ALU.add)
+                twin = sb.tile([P, N], F32, name="ex_twin%d" % i)
+                nc.vector.tensor_copy(twin[:], ex_win[i][:, :N])
+                nc.vector.tensor_tensor(pair[:], ex_win[i][:].indirect(n5_t[:]), twin[:], ALU.add)
             return pair
 
-        def divide(i, pair):
+        def finish(i, pair):
+            pieces = [half(0), half(1)] if i == LAST else [slice(0, N)]
             ratio = sb.tile([P, N], F32, name="ratio%d" % i)
-            pieces = 2 if i == 3 else 1
-            for h in range(pieces):
-                c = slice(h * N // pieces, (h + 1) * N // pieces)
-                entries = n6_t[:, c.start // 16 : c.stop // 16]
-                nc.vector.tensor_tensor(ratio[:, c], s_neg[i][:].indirect(entries), pair[:, c], ALU.mult)
-            return ratio
+            for columns in pieces:
+                looked_up = inv_win[i][:].indirect(entries(n6_t, columns))
+                nc.vector.tensor_tensor(ratio[:, columns], looked_up, pair[:, columns], ALU.mult)
+            name = "z_codes%d" % LAST if i == 0 else "result%d" % i
+            result = sb.tile([P, N], F32, name=name, align_bytes=64)
+            for columns in pieces:
+                nc.scalar.activation(result[:, columns], ratio[:, columns], ACT.Ln)
+                nc.sync.dma_start(out[i * P : (i + 1) * P, columns], result[:, columns])
 
-        def finish(i, ratio):
-            res = sb.tile([P, N], F32, name="z_codes3" if i == 0 else "res%d" % i, align_bytes=64)
-            pieces = 2 if i == 3 else 1
-            for h in range(pieces):
-                c = slice(h * N // pieces, (h + 1) * N // pieces)
-                nc.scalar.activation(res[:, c], ratio[:, c], ACT.Ln)
-                nc.sync.dma_start(out[i * P : (i + 1) * P, c], res[:, c])
-
-        ex5 = {}
-        banks = []
-        for i in range(4 + LAG):
-            if i < 4:
-                banks.append(scores(i))
-            if i in EARLY:
-                ex5[i] = fetch_ex5(i)
-            if i >= LAG:
-                inverse(i - LAG)
-        pairs = [add_pair(0, ex5.get(0))]
-        for i in range(4):
-            if i < 3:
-                pairs.append(add_pair(i + 1, ex5.get(i + 1)))
-            finish(i, divide(i, pairs[i]))
+        pairs = [add_pair(0)]
+        for i in range(BLOCKS):
+            if i < LAST:
+                pairs.append(add_pair(i + 1))
+            finish(i, pairs[i])

@@ -140,7 +140,7 @@ def tile_picked_hkqgaphingelse_none_p_kernel(
         w2_dealt = sb.tile([P, PACK, P, PACK], BF16, name="w2_dealt", align_bytes=64)
         w1_dealt = sb.tile([P, PACK, P, PACK], BF16, name="w1_dealt", align_bytes=64)
         for h in range(2):
-            nc.scalar.activation(*dealt_views(w2_dealt, w2_raw, h), ACT.Copy)
+            nc.scalar.copy(*dealt_views(w2_dealt, w2_raw, h))
         gb_half = sb.tile([P, PACK], F32, name="gb_half")
         nc.gpsimd.tensor_scalar(gb_half[:], gb_t[:], 0.5, 0.0, ALU.mult, ALU.add)
 
@@ -164,9 +164,9 @@ def tile_picked_hkqgaphingelse_none_p_kernel(
         b_twin = []
         for t in range(PACK):
             twin = sb.tile([P, N], F32, name="b_twin%d" % t)
-            nc.scalar.copy(b_win[t][:, :N], b_banks[t][:])
+            nc.scalar.activation(b_win[t][:, :N], b_banks[t][:], ACT.Copy)
             if t == 0:
-                nc.vector.tensor_copy(twin[:], b_win[t][:, :N])
+                nc.scalar.activation(twin[:], b_banks[t][:], ACT.Copy)
                 nc.scalar.activation(*dealt_views(w1_dealt, w1_raw, 1), ACT.Copy)
             else:
                 nc.sync.dma_start(twin[:], b_win[t][:, :N])

from contextlib import ExitStack

import concourse.mybir as mybir

F32 = mybir.dt.float32
BF16 = mybir.dt.bfloat16
I32 = mybir.dt.int32
U32 = mybir.dt.uint32
U16 = mybir.dt.uint16
U8 = mybir.dt.uint8
FP8X4 = mybir.dt.float8_e4m3fn_x4
ALU = mybir.AluOpType
ACT = mybir.ActivationFunctionType

P = 128
PACK = 4
T = 2048
N = 512
HALF = N // 2
PER_COLUMN = 16
QUADS = 4
BLOCKS = N // P
LAST = BLOCKS - 1
RUN = 4
SCORE_SCALE = 0.0625

B_SPARE = N
S_SPARE = PER_COLUMN

N4_TILE_ON_SCALAR = PACK - 1
N5_BLOCKS_ON_SCALAR = (0, LAST)

FLOPS = 3 * 2 * 512 * 512 * 512


def tile_picked_hkqgaphingelse_none_p_kernel(
    tc, x_words, x_scales, w1, w2, ga, gb, offs, two, n1, n2, n3, n4, n5, n6, out
):
    nc = tc.nc
    with ExitStack() as ctx:
        lists = ctx.enter_context(tc.tile_pool(name="lists", bufs=1))
        sb = ctx.enter_context(tc.tile_pool(name="sb", bufs=1))
        psum = ctx.enter_context(tc.psum_pool(name="psum", bufs=1))

        def half(h):
            return slice(h * HALF, (h + 1) * HALF)

        def entries(list_tile, columns):
            return list_tile[:, columns.start // PER_COLUMN : columns.stop // PER_COLUMN]

        def load_list(src, name):
            tile = lists.tile([P, N // PER_COLUMN], U16, name=name)
            nc.sync.dma_start(tile[:], src)
            return tile

        def load_weight_half(w, h, name):
            raw = sb.tile([P, PACK, HALF], F32, name=name)
            nc.sync.dma_start(raw[:], w.rearrange("(p j) c -> p j c", j=PACK)[:, :, half(h)])
            return raw

        def load_gain(g, name):
            tile = sb.tile([P, PACK], F32, name=name)
            nc.sync.dma_start(tile[:], g.rearrange("(p t) o -> p (t o)", t=PACK))
            return tile

        scales_two = sb.tile([P, T], U8, name="scales_two", align_bytes=64)
        nc.gpsimd.memset(scales_two[:].bitcast(I32), 0)
        scales_offs = sb.tile([P, T], U8, name="scales_offs", align_bytes=64)
        nc.gpsimd.memset(scales_offs[:].bitcast(I32), 0)
        xa_scale = sb.tile([P, N], U8, name="xa_scale", align_bytes=64)
        nc.gpsimd.memset(xa_scale[:].bitcast(I32), 0)
        for q in range(QUADS):
            rows = x_scales[0, 4 * q : 4 * q + 4, :].bitcast(I32)
            nc.scalar.dma_start(scales_two[32 * q : 32 * q + 4, :].bitcast(I32), rows)
        nc.scalar.dma_start(scales_offs[0:P:8, :].bitcast(I32), x_scales[0].bitcast(I32))

        two_t = load_list(two, "two_t")
        offs_t = load_list(offs, "offs_t")
        w2_raw = [load_weight_half(w2, h, "w2_raw%d" % h) for h in range(2)]
        words = sb.tile([P, T], I32, name="words", align_bytes=64)
        nc.sync.dma_start(words[:], x_words[0].rearrange("p n t -> p (n t)").bitcast(I32))
        w1_raw = [load_weight_half(w1, h, "w1_raw%d" % h) for h in range(2)]
        n3_t = load_list(n3, "n3_t")
        n4_t = load_list(n4, "n4_t")
        gb_t = load_gain(gb, "gb_t")
        ga_t = load_gain(ga, "ga_t")
        n1_t = load_list(n1, "n1_t")
        n2_t = load_list(n2, "n2_t")
        n5_t = load_list(n5, "n5_t")
        n6_t = load_list(n6, "n6_t")

        def window(name, spare):
            tile = sb.tile([P, N + spare], F32, name=name)
            nc.gpsimd.memset(tile[:, N:], 0.0)
            return tile

        b_win = [window("b_win%d" % t, B_SPARE) for t in range(PACK)]
        ex_win = [window("ex_win%d" % i, S_SPARE) for i in range(BLOCKS)]
        inv_win = [window("inv_win%d" % i, S_SPARE) for i in range(BLOCKS)]

        def dealt_views(dealt, raw, h):
            dst = dealt[:, :, h * (P // 2) : (h + 1) * (P // 2), :].rearrange("p t m j -> p m t j")
            src = raw[h][:].rearrange("p j (m t) -> p m t j", t=PACK)
            return dst, src

        def quantize_weight(dealt, name):
            codes = sb.tile([P, N], U32, name=name + "_codes", align_bytes=64)
            scale = sb.tile([P, N], U8, name=name + "_scale", align_bytes=64)
            for t in range(PACK):
                nc.vector.quantize_mx(
                    out=codes[:, t * P : (t + 1) * P].bitcast(FP8X4),
                    scales=scale[:, t * P : (t + 1) * P],
                    in_=dealt[:, t, :, :].rearrange("p m j -> p (m j)"),
                )
            return codes, scale

        def product(bank_name, lhs_codes, lhs_scale, rhs_codes, rhs_scale):
            bank = psum.tile([P, N], F32, name=bank_name)
            nc.tensor.matmul_mx(
                out=bank[:],
                lhsT=lhs_codes.bitcast(FP8X4),
                lhsT_scale=lhs_scale,
                rhs=rhs_codes.bitcast(FP8X4),
                rhs_scale=rhs_scale,
                start=True,
                stop=True,
            )
            return bank

        def subtract_and_round(dst, in0, in1):
            nc.vector.tensor_tensor(
                dst.rearrange("p (r i t) -> p r t i", i=RUN, t=PACK),
                in0.rearrange("p t (r i) -> p r t i", i=RUN),
                in1.rearrange("p t (r i) -> p r t i", i=RUN),
                ALU.subtract,
            )

        xb_scale = sb.tile([P, N], U8, name="xb_scale", align_bytes=64)
        nc.vector.tensor_copy(xb_scale[:], scales_two[:].indirect(two_t[:]))
        w2_dealt = sb.tile([P, PACK, P, PACK], BF16, name="w2_dealt", align_bytes=64)
        w1_dealt = sb.tile([P, PACK, P, PACK], BF16, name="w1_dealt", align_bytes=64)
        for h in range(2):
            nc.scalar.copy(*dealt_views(w2_dealt, w2_raw, h))
        gb_half = sb.tile([P, PACK], F32, name="gb_half")
        nc.gpsimd.tensor_scalar(gb_half[:], gb_t[:], 0.5, 0.0, ALU.mult, ALU.add)

        xa_picked = sb.tile([P, N], U8, name="xa_picked", align_bytes=64)
        nc.vector.tensor_copy(xa_picked[:], scales_offs[:].indirect(offs_t[:]))
        for r in range(4):
            nc.sync.dma_start(xa_scale[r:P:32, :].bitcast(I32), xa_picked[8 * r : P : 32, :].bitcast(I32))
        w2_codes, w2_scale = quantize_weight(w2_dealt, "w2")
        xb_codes = sb.tile([P, N], U32, name="xb_codes", align_bytes=64)
        nc.vector.tensor_copy(xb_codes[:], words[:].bitcast(U32).indirect(two_t[:]))
        xa_codes = sb.tile([P, N], U32, name="xa_codes", align_bytes=64)
        nc.vector.tensor_copy(xa_codes[:], words[:].bitcast(U32).indirect(offs_t[:]))

        b_banks = []
        for t in range(PACK):
            tile_cols = slice(t * P, (t + 1) * P)
            b_banks.append(
                product("bank%d" % t, w2_codes[:, tile_cols], w2_scale[:, tile_cols], xb_codes[:], xb_scale[:])
            )
        nc.vector.tensor_copy(*dealt_views(w1_dealt, w1_raw, 0))
        b_twin = []
        for t in range(PACK):
            twin = sb.tile([P, N], F32, name="b_twin%d" % t)
            nc.scalar.activation(b_win[t][:, :N], b_banks[t][:], ACT.Copy)
            if t == 0:
                nc.scalar.activation(twin[:], b_banks[t][:], ACT.Copy)
                nc.scalar.activation(*dealt_views(w1_dealt, w1_raw, 1), ACT.Copy)
            else:
                nc.sync.dma_start(twin[:], b_win[t][:, :N])
            b_twin.append(twin)

        d3 = sb.tile([P, PACK, N], F32, name="d3")
        d4 = sb.tile([P, PACK, N], F32, name="d4")
        down = sb.tile([P, PACK, N], F32, name="down")
        up = sb.tile([P, PACK, N], F32, name="up")
        b4 = sb.tile([P, N], F32, name="b4")

        def differences(t):
            nc.vector.tensor_tensor(d3[:, t, :], b_win[t][:].indirect(n3_t[:]), b_twin[t][:], ALU.subtract)
            looked_up = b4[:] if t == N4_TILE_ON_SCALAR else b_win[t][:].indirect(n4_t[:])
            nc.vector.tensor_tensor(d4[:, t, :], looked_up, b_twin[t][:], ALU.subtract)

        def hinges(t):
            nc.vector.tensor_scalar(down[:, t, :], d3[:, t, :], 0.0, gb_t[:, t : t + 1], ALU.min, ALU.mult)
            nc.vector.tensor_scalar(up[:, t, :], d4[:, t, :], 0.0, gb_half[:, t : t + 1], ALU.max, ALU.mult)

        w1_codes, w1_scale = quantize_weight(w1_dealt, "w1")
        differences(0)
        nc.scalar.activation(b4[:], b_win[N4_TILE_ON_SCALAR][:].indirect(n4_t[:]), ACT.Copy)

        a_win = []
        for t in range(PACK):
            tile_cols = slice(t * P, (t + 1) * P)
            bank = product(
                "bank%d" % (PACK + t), w1_codes[:, tile_cols], w1_scale[:, tile_cols], xa_codes[:], xa_scale[:]
            )
            weighted = sb.tile([P, N], F32, name="a_win%d" % t)
            nc.scalar.activation(weighted[:], bank[:], ACT.Copy, scale=ga_t[:, t : t + 1])
            a_win.append(weighted)
        a1 = [sb.tile([P, PACK, HALF], F32, name="a1_%d" % h) for h in range(2)]
        a2 = [sb.tile([P, PACK, HALF], F32, name="a2_%d" % h) for h in range(2)]
        for h in range(2):
            for t in range(PACK):
                nc.scalar.activation(a1[h][:, t, :], a_win[t][:].indirect(entries(n1_t, half(h))), ACT.Copy)
                nc.scalar.activation(a2[h][:, t, :], a_win[t][:].indirect(entries(n2_t, half(h))), ACT.Copy)

        for t in range(1, PACK):
            differences(t)
            hinges(t - 1)
        hinges(PACK - 1)

        z2_codes = sb.tile([P, N], U32, name="z2_codes", align_bytes=64)
        z2_scale = sb.tile([P, N], U8, name="z2_scale", align_bytes=64)
        z2_bf = [sb.tile([P, HALF * PACK], BF16, name="z2_bf%d" % h, align_bytes=64) for h in range(2)]
        z_bf = [sb.tile([P, P * PACK], BF16, name="z_bf%d" % i, align_bytes=64) for i in range(BLOCKS)]
        z_codes = [sb.tile([P, P], U32, name="z_codes%d" % i, align_bytes=64) for i in range(BLOCKS)]
        z_scale = [sb.tile([P, P], U8, name="z_scale%d" % i, align_bytes=64) for i in range(BLOCKS)]

        def round_z(i):
            h, within = divmod(i * P, HALF)
            columns = slice(within, within + P)
            subtract_and_round(z_bf[i][:], a1[h][:, :, columns], a2[h][:, :, columns])

        def quantize_z(i):
            nc.vector.quantize_mx(out=z_codes[i][:].bitcast(FP8X4), scales=z_scale[i][:], in_=z_bf[i][:])

        for h in range(2):
            subtract_and_round(z2_bf[h][:], up[:, :, half(h)], down[:, :, half(h)])
        round_z(0)
        for h in range(2):
            nc.vector.quantize_mx(out=z2_codes[:, half(h)].bitcast(FP8X4), scales=z2_scale[:, half(h)], in_=z2_bf[h][:])
        for i in range(1, BLOCKS):
            quantize_z(i - 1)
            round_z(i)
        quantize_z(LAST)

        s_banks = []
        ex5 = {}
        for i in range(BLOCKS + 1):
            if i < BLOCKS:
                s_banks.append(product("bank%d" % i, z_codes[i][:], z_scale[i][:], z2_codes[:], z2_scale[:]))
                nc.scalar.activation(ex_win[i][:, :N], s_banks[i][:], ACT.Exp, scale=SCORE_SCALE)
            if i in N5_BLOCKS_ON_SCALAR:
                ex5[i] = sb.tile([P, N], F32, name="ex5_%d" % i)
                nc.scalar.activation(ex5[i][:], ex_win[i][:].indirect(n5_t[:]), ACT.Copy)
            if i >= 1:
                nc.scalar.activation(inv_win[i - 1][:, :N], s_banks[i - 1][:], ACT.Exp, scale=-SCORE_SCALE)

        def add_pair(i):
            pair = sb.tile([P, N], F32, name="pair%d" % i)
            if i in N5_BLOCKS_ON_SCALAR:
                nc.vector.tensor_tensor(pair[:], ex_win[i][:, :N], ex5[i][:], ALU.add)
            else:
                twin = sb.tile([P, N], F32, name="ex_twin%d" % i)
                nc.vector.tensor_copy(twin[:], ex_win[i][:, :N])
                nc.vector.tensor_tensor(pair[:], ex_win[i][:].indirect(n5_t[:]), twin[:], ALU.add)
            return pair

        def finish(i, pair):
            pieces = [half(0), half(1)] if i == LAST else [slice(0, N)]
            ratio = sb.tile([P, N], F32, name="ratio%d" % i)
            for columns in pieces:
                looked_up = inv_win[i][:].indirect(entries(n6_t, columns))
                nc.vector.tensor_tensor(ratio[:, columns], looked_up, pair[:, columns], ALU.mult)
            name = "z_codes%d" % LAST if i == 0 else "result%d" % i
            result = sb.tile([P, N], F32, name=name, align_bytes=64)
            for columns in pieces:
                nc.scalar.activation(result[:, columns], ratio[:, columns], ACT.Ln)
                nc.sync.dma_start(out[i * P : (i + 1) * P, columns], result[:, columns])

        pairs = [add_pair(0)]
        for i in range(BLOCKS):
            if i < LAST:
                pairs.append(add_pair(i + 1))
            finish(i, pairs[i])
